import numpy as np
import ml_dtypes


def mxq(x, axis, fmt="e4m3"):
    dtype, down = {"e4m3": (ml_dtypes.float8_e4m3fn, 7), "e5m2": (ml_dtypes.float8_e5m2, 14)}[fmt]
    v = np.moveaxis(np.asarray(x, np.float32).astype(ml_dtypes.bfloat16).astype(np.float64), axis, -1)
    blocks = v.reshape(v.shape[:-1] + (-1, 32))
    amax = np.abs(blocks).max(-1, keepdims=True)
    byte = np.maximum(np.where(amax > 0, np.frexp(amax)[1] - 1 + 127, 0) - down, 1)
    scale = np.exp2(byte - 127.0)
    codes = (blocks / scale).astype(np.float32).astype(dtype).astype(np.float64)
    return np.moveaxis((codes * scale).reshape(v.shape), -1, axis)


WIDE = False


def mx_kscale(k):
    if not WIDE:
        return np.ones(k)
    levels = np.array([10, -10, 5, -5, 0])
    if k % 512:
        return np.exp2(np.random.permutation(np.resize(levels, k // 32))).repeat(32)
    a = np.empty((k // 512, 16))
    for p in range(k // 512):
        a[p, :8] = np.random.permutation(np.resize(levels, 8))
        for g in range(8):
            far = levels[np.abs(levels - a[p, g]) >= 10]
            a[p, g + 8] = far[np.random.randint(len(far))]
    return np.exp2(a.ravel()).repeat(32)


def f64(x):
    return np.asarray(x).astype(np.float64)


def striped8(idx):
    return np.asarray(idx).reshape(8, -1, 16).transpose(0, 2, 1).reshape(128, -1).astype(np.uint16)


def unstriped8(offs):
    return offs.reshape(8, 16, -1).transpose(0, 2, 1).reshape(8, -1).astype(np.int64)


def pick8(x, idx, run):
    r = np.arange(len(x))
    return x[r[:, None], idx[r % (8 * run) // run]]


E2M1 = np.array([0.0, 0.5, 1.0, 1.5, 2.0, 3.0, 4.0, 6.0, -0.0, -0.5, -1.0, -1.5, -2.0, -3.0, -4.0, -6.0])


def pack_weight(w, fmt):
    k, n = w.shape
    w = f64(np.asarray(w, np.float32).astype(ml_dtypes.bfloat16)).reshape(k // 32, 32, n)
    amax = np.abs(w).max(1)
    if fmt == "e4m3":
        byte = np.frexp(amax)[1] - 1 + 127 - 7
    else:
        mant, ex = np.frexp(amax / 6.0)
        byte = np.where(mant > 0.5, ex, ex - 1) + 127
    byte = np.clip(np.where(amax > 0, byte, 1), 1, 254)
    scaled = (w * np.exp2(127.0 - byte)[:, None, :]).reshape(k, n).astype(np.float32)
    by_word = np.ascontiguousarray(scaled.reshape(k // 512, 128, 4, n).transpose(0, 1, 3, 2))
    if fmt == "e4m3":
        words = by_word.astype(ml_dtypes.float8_e4m3fn).view(np.uint8)
    else:
        c = by_word.astype(ml_dtypes.float4_e2m1fn).view(np.uint8) & 0xF
        words = (c[..., 0::2] | (c[..., 1::2] << 4)).reshape(k // 512, 128, 2 * n)
    return np.ascontiguousarray(words), np.ascontiguousarray(byte.astype(np.uint8).reshape(k // 512, 16, n))


def unpack_weight(words, scales, fmt):
    g, _, n = scales.shape
    words = np.ascontiguousarray(words).reshape(g, 128, n, -1)
    if fmt == "e4m3":
        vals = words.view(ml_dtypes.float8_e4m3fn).astype(np.float64)
    else:
        nib = np.empty((g, 128, n, 4), np.uint8)
        nib[..., 0::2] = words & 0xF
        nib[..., 1::2] = words >> 4
        vals = E2M1[nib]
    vals = vals * np.repeat(np.exp2(scales.astype(np.float64) - 127.0), 8, axis=1)[..., None]
    return vals.transpose(0, 1, 3, 2).reshape(g * 512, n)


D, V, Q, I, G = 512, 2048, 128, 512, 64


def setup_inputs():
    n = np.random.standard_normal
    idx = np.stack([np.random.permutation(V)[:I] for _ in range(8)])
    fd = mx_kscale(D)
    vocp = pack_weight(n((D, V)) / fd[:, None], "e2m1")
    return {
        "hid": (n((D, Q)) * 1.0 / np.sqrt(D) * fd[:, None]).astype(np.float32),
        "voc_words": vocp[0],
        "voc_scales": vocp[1],
        "aim": (np.random.uniform(0.3, 1.7, (Q, G))).astype(np.float32),
        "dhid": (n((D, Q)) * 1.0 / np.sqrt(D) * fd[:, None]).astype(np.float32),
        "base": (0.5 * n((Q, V))).astype(np.float32),
        "offs": striped8(idx),
    }


def reference(hid, voc_words, voc_scales, aim, dhid, base, offs):
    idx = unstriped8(offs)
    vocu = unpack_weight(voc_words, voc_scales, "e2m1")
    hidq = mxq(f64(hid), 0, "e4m3")
    a = hidq.T @ vocu
    dhidq = mxq(f64(dhid), 0, "e4m3")
    ta = dhidq.T @ vocu
    m1 = np.max(a, axis=1, keepdims=True)
    p = np.exp(a - m1)
    z = np.sum(p, axis=1, keepdims=True)
    px = np.exp(pick8(a, idx, 16) - m1)
    s1g = px.reshape(Q, G, I // G).sum(axis=2)
    u1 = s1g / z * 256.0 - f64(aim)
    du1 = u1 * 2.0
    ds1g = du1 * 256.0 / z
    r1 = np.repeat(ds1g, I // G, axis=1)
    dz = np.sum(du1 * 256.0 * s1g / np.square(z) * (-1.0), axis=1, keepdims=True)
    xp = ta * p
    xz = np.sum(xp, axis=1, keepdims=True)
    xpx = pick8(ta, idx, 16) * px
    xs1g = xpx.reshape(Q, G, I // G).sum(axis=2)
    xu1 = (xs1g - xz * s1g / z) / z * 256.0
    xdu1 = xu1 * 2.0
    xds1g = (xdu1 * 256.0 - xz * du1 * 256.0 / z) / z
    xr1 = np.repeat(xds1g, I // G, axis=1)
    xdz = np.sum((xdu1 * 256.0 * s1g + xs1g * du1 * 256.0 - xz * z * 2.0 * du1 * 256.0 * s1g / np.square(z)) / np.square(z) * (-1.0), axis=1, keepdims=True)
    xe2 = xr1 * px + xpx * r1
    xs2 = np.zeros((Q, V))
    xs2[np.arange(Q)[:, None], idx[np.arange(Q) % 128 // 16]] = xe2
    xda = xdz * p + xp * dz + xs2
    y = xda + f64(base)
    return y

@@ -1,0 +1,249 @@
+from contextlib import ExitStack
+
+import concourse.mybir as mybir
+from concourse.masks import make_identity
+
+D, V, Q, SLOTS, G = 512, 2048, 128, 512, 64
+GROUP = SLOTS // G
+FLOPS = 2 * 2 * D * Q * V
+
+F32 = mybir.dt.float32
+BF16 = mybir.dt.bfloat16
+U32 = mybir.dt.uint32
+I32 = mybir.dt.int32
+U16 = mybir.dt.uint16
+U8 = mybir.dt.uint8
+FP8X4 = mybir.dt.float8_e4m3fn_x4
+FP4X4 = mybir.dt.float4_e2m1fn_x4
+ALU = mybir.AluOpType
+ACT = mybir.ActivationFunctionType
+AX = mybir.AxisListType
+
+P = 128
+PACK = 4
+BANK = 512
+CHUNKS = V // BANK
+BLOCKS = BANK // P
+
+
+def tile_attend_hvgroupaims_heads_kernel(tc, hid, voc_words, voc_scales, aim, dhid, base, offs, out):
+    nc = tc.nc
+    with ExitStack() as ctx:
+        sb = ctx.enter_context(tc.tile_pool(name="sb", bufs=1))
+        ps = ctx.enter_context(tc.psum_pool(name="ps", bufs=1))
+
+        def cols(c):
+            return slice(c * BANK, (c + 1) * BANK)
+
+        def col(t, c):
+            return t[:, c : c + 1]
+
+        def grouped(ap):
+            return ap.rearrange("p (g j) -> p g j", j=GROUP)
+
+        def spread(ap):
+            return ap.unsqueeze(2).to_broadcast([P, G, GROUP])
+
+        voc_plane = sb.tile([P, V], U8, align_bytes=64)
+        nc.vector.memset(voc_plane[:].bitcast(I32), 0)
+        warm = sb.tile([P, 1], F32)
+        nc.vector.memset(warm[:], 0.0)
+        warm_out = sb.tile([P, 1], F32)
+        nc.scalar.activation(warm_out[:], warm[:], ACT.Exp)
+
+        hid_raw = sb.tile([P, PACK, Q], F32)
+        nc.sync.dma_start(hid_raw[:], hid.rearrange("(p t) q -> p t q", t=PACK))
+        for quad in range(4):
+            nc.sync.dma_start(
+                voc_plane[32 * quad : 32 * quad + 4, :].bitcast(I32),
+                voc_scales[0, 4 * quad : 4 * quad + 4, :].bitcast(I32),
+            )
+        words = [sb.tile([P, 2 * BANK], U8, name=f"words{c}", align_bytes=64) for c in range(CHUNKS)]
+        for c in range(CHUNKS):
+            nc.sync.dma_start(words[c][:].bitcast(I32), voc_words[0, :, 2 * c * BANK : 2 * (c + 1) * BANK].bitcast(I32))
+        dhid_raw = sb.tile([P, PACK, Q], F32)
+        nc.sync.dma_start(dhid_raw[:], dhid.rearrange("(p t) q -> p t q", t=PACK))
+        offsets = sb.tile([P, SLOTS // 16], U16)
+        nc.sync.dma_start(offsets[:], offs)
+        aim_sb = sb.tile([P, G], F32)
+        nc.sync.dma_start(aim_sb[:], aim)
+        base_sb = [sb.tile([P, BANK], F32, name=f"base{c}") for c in range(CHUNKS)]
+        for c in range(CHUNKS):
+            nc.sync.dma_start(base_sb[c][:], base[:, cols(c)])
+
+        ident = sb.tile([P, P], F32)
+        make_identity(nc, ident[:])
+        xs2 = sb.tile([P, V], F32)
+        nc.vector.memset(xs2[:], 0.0)
+        lin_consts = sb.tile([P, 2], F32)
+        nc.vector.memset(lin_consts[:, 0:1], 256.0)
+        nc.vector.memset(lin_consts[:, 1:2], 512.0)
+        sq_consts = sb.tile([P, 2], F32)
+        nc.vector.memset(sq_consts[:, 0:1], -512.0)
+        nc.vector.memset(sq_consts[:, 1:2], 131072.0)
+        xs_ext = sb.tile([P, G + 2], F32)
+        nc.vector.memset(xs_ext[:, G : G + 2], -1.0)
+
+        def interleaved(name):
+            return sb.tile([P, Q * PACK], BF16, name=name, align_bytes=64)
+
+        def as_written(t):
+            return t[:].rearrange("p (c i t) -> p c t i", i=4, t=PACK)
+
+        def as_read(raw):
+            return raw[:].rearrange("p t (c i) -> p c t i", i=4)
+
+        def quantise(name, bf):
+            codes = sb.tile([P, Q], U32, name=name + "_codes", align_bytes=64)
+            plane = sb.tile([P, Q], U8, name=name + "_plane", align_bytes=64)
+            nc.vector.quantize_mx(out=codes[:].bitcast(FP8X4), scales=plane[:], in_=bf[:])
+            return codes, plane
+
+        hid_bf = interleaved("hid_bf")
+        nc.vector.tensor_copy(as_written(hid_bf), as_read(hid_raw))
+        dhid_bf = interleaved("dhid_bf")
+        nc.scalar.copy(as_written(dhid_bf), as_read(dhid_raw))
+        hid_q = quantise("hid", hid_bf)
+        dhid_q = quantise("dhid", dhid_bf)
+
+        def scores(name, operand, c):
+            bank = ps.tile([P, BANK], F32, name=f"{name}{c}", tag=f"{name}{c}")
+            codes, plane = operand
+            nc.tensor.matmul_mx(
+                out=bank[:],
+                lhsT=codes[:].bitcast(FP8X4),
+                lhsT_scale=plane[:],
+                rhs=words[c][:].bitcast(FP4X4),
+                rhs_scale=voc_plane[:, cols(c)],
+                start=True,
+                stop=True,
+            )
+            return bank
+
+        a_ps = [scores("left", hid_q, c) for c in range(CHUNKS)]
+        ta_ps = [scores("right", dhid_q, c) for c in range(CHUNKS)]
+
+        a_sb = sb.tile([P, V], F32)
+        cmax = sb.tile([P, CHUNKS], F32)
+        neg_cmax = sb.tile([P, CHUNKS], F32)
+        csum = sb.tile([P, CHUNKS], F32)
+        p = [sb.tile([P, BANK], F32, name=f"p{c}") for c in range(CHUNKS)]
+        for c in range(CHUNKS):
+            nc.vector.tensor_scalar(a_sb[:, cols(c)], a_ps[c][:], 1.0, None, ALU.mult, ALU.max, accum_out=col(cmax, c))
+            nc.gpsimd.tensor_scalar(col(neg_cmax, c), col(cmax, c), -1.0, 0.0, ALU.mult, ALU.add)
+            nc.scalar.activation(p[c][:], a_sb[:, cols(c)], ACT.Exp, bias=col(neg_cmax, c), accum_out=col(csum, c))
+        neg_max = sb.tile([P, 1], F32)
+        nc.vector.tensor_reduce(neg_max[:], cmax[:], AX.X, ALU.max, negate=True)
+        ax = sb.tile([P, SLOTS], F32)
+        nc.vector.tensor_copy(ax[:], a_sb[:].indirect(offsets[:]))
+        fac = sb.tile([P, CHUNKS], F32)
+        nc.scalar.activation(fac[:], cmax[:], ACT.Exp, bias=neg_max[:])
+        px = sb.tile([P, SLOTS], F32)
+        nc.scalar.activation(px[:], ax[:], ACT.Exp, bias=neg_max[:])
+
+        turned = [ps.tile([P, BANK], F32, name=f"turned{c}", tag=f"left{c}") for c in range(CHUNKS)]
+
+        def add_turned(c, term, first=False, last=False):
+            for j in range(BLOCKS):
+                block = slice(j * P, (j + 1) * P)
+                nc.tensor.matmul(
+                    turned[c][:, block], lhsT=term[:, block], rhs=ident[:], is_transpose=True,
+                    start=(first and j == 0), stop=(last and j == BLOCKS - 1),
+                )
+
+        for c in range(CHUNKS):
+            add_turned(c, base_sb[c], first=True)
+
+        xp = [sb.tile([P, BANK], F32, name=f"xp{c}") for c in range(CHUNKS)]
+        xsum = sb.tile([P, CHUNKS], F32)
+        ta_sb = sb.tile([P, V], F32)
+
+        def weigh(c):
+            nc.vector.scalar_tensor_tensor(
+                xp[c][:], ta_ps[c][:], 1.0, p[c][:], ALU.mult, ALU.mult, accum_out=col(xsum, c)
+            )
+
+        def copy_ta(c):
+            nc.scalar.copy(ta_sb[:, cols(c)], ta_ps[c][:])
+
+        def dot(name, total, x, scalar, y):
+            terms = sb.tile([P, x.shape[1]], F32, name=name)
+            nc.vector.scalar_tensor_tensor(terms[:], x, scalar, y, ALU.mult, ALU.mult, accum_out=total)
+
+        z = sb.tile([P, 1], F32)
+        rz = sb.tile([P, 1], F32)
+        s1g = sb.tile([P, G], F32)
+        lin = sb.tile([P, 2], F32)
+        sq = sb.tile([P, 2], F32)
+        crz, k, nk2, kc = col(lin, 0), col(lin, 1), col(sq, 0), col(sq, 1)
+        u = sb.tile([P, G], F32)
+        w_ext = sb.tile([P, G + 2], F32)
+        w = w_ext[:, 0:G]
+        dz = sb.tile([P, 1], F32)
+        mu = sb.tile([P, 1], F32)
+        dz_fac = sb.tile([P, CHUNKS], F32)
+        wm = sb.tile([P, G], F32)
+
+        copy_ta(3)
+        copy_ta(2)
+        weigh(0)
+        copy_ta(0)
+        dot("z_terms", z[:], csum[:], 1.0, fac[:])
+        weigh(1)
+        copy_ta(1)
+        nc.vector.reciprocal(rz[:], z[:])
+        nc.vector.tensor_reduce(s1g[:], grouped(px[:]), AX.X, ALU.add)
+        nc.vector.tensor_scalar(lin[:], lin_consts[:], rz[:], None, ALU.mult)
+        nc.vector.tensor_scalar(sq[:], sq_consts[:], rz[:], rz[:], ALU.mult, ALU.mult)
+        weigh(2)
+        nc.vector.scalar_tensor_tensor(u[:], s1g[:], crz, aim_sb[:], ALU.mult, ALU.subtract)
+        nc.vector.scalar_tensor_tensor(w, s1g[:], k, aim_sb[:], ALU.mult, ALU.subtract)
+        weigh(3)
+        dot("dz_terms", dz[:], u[:], nk2, s1g[:])
+        dot("mu_terms", mu[:], xsum[:], rz[:], fac[:])
+        nc.vector.tensor_scalar(dz_fac[:], fac[:], dz[:], None, ALU.mult)
+        xpx = sb.tile([P, SLOTS], F32)
+        nc.vector.tensor_tensor(xpx[:], ta_sb[:].indirect(offsets[:]), px[:], ALU.mult)
+        dot("u_terms", col(w_ext, G), u[:], mu[:], s1g[:])
+        dot("w_terms", col(w_ext, G + 1), w, mu[:], s1g[:])
+        nc.vector.tensor_scalar(wm[:], w, mu[:], k, ALU.mult, ALU.mult)
+
+        for c in range(CHUNKS):
+            term = sb.tile([P, BANK], F32, name=f"dz_term{c}")
+            nc.scalar.activation(term[:], xp[c][:], ACT.Copy, scale=col(dz_fac, c))
+            add_turned(c, term)
+
+        nc.vector.tensor_reduce(xs_ext[:, 0:G], grouped(xpx[:]), AX.X, ALU.add)
+        e2 = sb.tile([P, SLOTS], F32)
+        nc.vector.scalar_tensor_tensor(grouped(e2[:]), grouped(xpx[:]), k, spread(u[:]), ALU.mult, ALU.mult)
+        xdz = sb.tile([P, 1], F32)
+        dot("xdz_terms", xdz[:], xs_ext[:], nk2, w_ext[:])
+        xr = sb.tile([P, G], F32)
+        nc.vector.scalar_tensor_tensor(xr[:], xs_ext[:, 0:G], kc, wm[:], ALU.mult, ALU.subtract)
+        xdz_fac = sb.tile([P, CHUNKS], F32)
+        nc.vector.tensor_scalar(xdz_fac[:], fac[:], xdz[:], None, ALU.mult)
+        e1 = sb.tile([P, SLOTS], F32)
+        nc.vector.tensor_tensor(grouped(e1[:]), grouped(px[:]), spread(xr[:]), ALU.mult)
+        nc.vector.tensor_tensor(xs2[:].indirect(offsets[:]), e1[:], e2[:], ALU.add)
+
+        def last_term(c):
+            term = sb.tile([P, BANK], F32, name=f"xdz_term{c}")
+            nc.scalar.activation(term[:], p[c][:], ACT.Copy, scale=col(xdz_fac, c))
+            add_turned(c, term, last=True)
+
+        def finish(c):
+            held = sb.tile([P, BANK], F32, name=f"held{c}")
+            nc.scalar.copy(held[:], turned[c][:])
+            dense = ps.tile([P, BANK], F32, name=f"dense{c}", tag=f"right{c}")
+            for j in range(BLOCKS):
+                block = slice(j * P, (j + 1) * P)
+                nc.tensor.transpose(dense[:, block], held[:, block], ident[:])
+            result = sb.tile([P, BANK], F32, name=f"result{c}")
+            nc.vector.tensor_tensor(result[:], dense[:], xs2[:, cols(c)], ALU.add)
+            nc.sync.dma_start(out[:, cols(c)], result[:])
+
+        last_term(0)
+        for c in range(CHUNKS):
+            if c + 1 < CHUNKS:
+                last_term(c + 1)
+            finish(c)

@@ -47,7 +47,7 @@ def tile_attend_hvgroupaims_heads_kernel(tc, hid, voc_words, voc_scales, aim, dh
         voc_plane = sb.tile([P, V], U8, align_bytes=64)
         nc.vector.memset(voc_plane[:].bitcast(I32), 0)
         warm = sb.tile([P, 1], F32)
-        nc.vector.memset(warm[:], 0.0)
+        nc.gpsimd.memset(warm[:], 0.0)
         warm_out = sb.tile([P, 1], F32)
         nc.scalar.activation(warm_out[:], warm[:], ACT.Exp)
 
@@ -65,7 +65,7 @@ def tile_attend_hvgroupaims_heads_kernel(tc, hid, voc_words, voc_scales, aim, dh
         nc.sync.dma_start(dhid_raw[:], dhid.rearrange("(p t) q -> p t q", t=PACK))
         offsets = sb.tile([P, SLOTS // 16], U16)
         nc.sync.dma_start(offsets[:], offs)
-        aim_sb = sb.tile([P, G], F32)
+        aim_sb = sb.tile([P, G], F32, tag="aim")
         nc.sync.dma_start(aim_sb[:], aim)
         base_sb = [sb.tile([P, BANK], F32, name=f"base{c}") for c in range(CHUNKS)]
         for c in range(CHUNKS):
@@ -75,14 +75,13 @@ def tile_attend_hvgroupaims_heads_kernel(tc, hid, voc_words, voc_scales, aim, dh
         make_identity(nc, ident[:])
         xs2 = sb.tile([P, V], F32)
         nc.vector.memset(xs2[:], 0.0)
-        lin_consts = sb.tile([P, 2], F32)
-        nc.vector.memset(lin_consts[:, 0:1], 256.0)
-        nc.vector.memset(lin_consts[:, 1:2], 512.0)
+        lin_consts = sb.tile([P, 3], F32)
+        nc.gpsimd.memset(lin_consts[:, 0:1], 256.0)
+        nc.gpsimd.memset(lin_consts[:, 1:2], 512.0)
+        nc.gpsimd.memset(lin_consts[:, 2:3], -1.0)
         sq_consts = sb.tile([P, 2], F32)
-        nc.vector.memset(sq_consts[:, 0:1], -512.0)
-        nc.vector.memset(sq_consts[:, 1:2], 131072.0)
-        xs_ext = sb.tile([P, G + 2], F32)
-        nc.vector.memset(xs_ext[:, G : G + 2], -1.0)
+        nc.gpsimd.memset(sq_consts[:, 0:1], -512.0)
+        nc.gpsimd.memset(sq_consts[:, 1:2], 131072.0)
 
         def interleaved(name):
             return sb.tile([P, Q * PACK], BF16, name=name, align_bytes=64)
@@ -123,25 +122,28 @@ def tile_attend_hvgroupaims_heads_kernel(tc, hid, voc_words, voc_scales, aim, dh
         a_ps = [scores("left", hid_q, c) for c in range(CHUNKS)]
         ta_ps = [scores("right", dhid_q, c) for c in range(CHUNKS)]
 
-        a_sb = sb.tile([P, V], F32)
+        a_sb = sb.tile([P, V], F32, tag="scores")
         cmax = sb.tile([P, CHUNKS], F32)
-        neg_cmax = sb.tile([P, CHUNKS], F32)
+        neg_run = sb.tile([P, CHUNKS], F32)
         csum = sb.tile([P, CHUNKS], F32)
         p = [sb.tile([P, BANK], F32, name=f"p{c}") for c in range(CHUNKS)]
         for c in range(CHUNKS):
             nc.vector.tensor_scalar(a_sb[:, cols(c)], a_ps[c][:], 1.0, None, ALU.mult, ALU.max, accum_out=col(cmax, c))
-            nc.gpsimd.tensor_scalar(col(neg_cmax, c), col(cmax, c), -1.0, 0.0, ALU.mult, ALU.add)
-            nc.scalar.activation(p[c][:], a_sb[:, cols(c)], ACT.Exp, bias=col(neg_cmax, c), accum_out=col(csum, c))
-        neg_max = sb.tile([P, 1], F32)
-        nc.vector.tensor_reduce(neg_max[:], cmax[:], AX.X, ALU.max, negate=True)
-        ax = sb.tile([P, SLOTS], F32)
+            if c == 0:
+                nc.gpsimd.tensor_scalar(col(neg_run, c), col(cmax, c), -1.0, 0.0, ALU.mult, ALU.add)
+            else:
+                nc.gpsimd.tensor_scalar(col(neg_run, c), col(cmax, c), -1.0, col(neg_run, c - 1), ALU.mult, ALU.min)
+            nc.scalar.activation(p[c][:], a_sb[:, cols(c)], ACT.Exp, bias=col(neg_run, c), accum_out=col(csum, c))
+        neg_max = col(neg_run, CHUNKS - 1)
+        ax = sb.tile([P, SLOTS], F32, tag="ax")
         nc.vector.tensor_copy(ax[:], a_sb[:].indirect(offsets[:]))
         fac = sb.tile([P, CHUNKS], F32)
-        nc.scalar.activation(fac[:], cmax[:], ACT.Exp, bias=neg_max[:])
+        nc.scalar.activation(fac[:], neg_run[:], ACT.Exp, bias=neg_max, scale=-1.0)
         px = sb.tile([P, SLOTS], F32)
-        nc.scalar.activation(px[:], ax[:], ACT.Exp, bias=neg_max[:])
+        nc.scalar.activation(px[:], ax[:], ACT.Exp, bias=neg_max)
 
-        turned = [ps.tile([P, BANK], F32, name=f"turned{c}", tag=f"left{c}") for c in range(CHUNKS)]
+        direct = CHUNKS - 1
+        turned = [ps.tile([P, BANK], F32, name=f"turned{c}", tag=f"left{c}") for c in range(direct)]
 
         def add_turned(c, term, first=False, last=False):
             for j in range(BLOCKS):
@@ -151,14 +153,16 @@ def tile_attend_hvgroupaims_heads_kernel(tc, hid, voc_words, voc_scales, aim, dh
                     start=(first and j == 0), stop=(last and j == BLOCKS - 1),
                 )
 
-        for c in range(CHUNKS):
+        for c in range(direct):
             add_turned(c, base_sb[c], first=True)
 
-        xp = [sb.tile([P, BANK], F32, name=f"xp{c}") for c in range(CHUNKS)]
+        xp_tags = ["xp0", "ax", "aim", "us_terms"]
+        xp = {}
         xsum = sb.tile([P, CHUNKS], F32)
-        ta_sb = sb.tile([P, V], F32)
+        ta_sb = sb.tile([P, V], F32, tag="scores")
 
         def weigh(c):
+            xp[c] = sb.tile([P, BANK], F32, name=f"xp{c}", tag=xp_tags[c])
             nc.vector.scalar_tensor_tensor(
                 xp[c][:], ta_ps[c][:], 1.0, p[c][:], ALU.mult, ALU.mult, accum_out=col(xsum, c)
             )
@@ -167,83 +171,105 @@ def tile_attend_hvgroupaims_heads_kernel(tc, hid, voc_words, voc_scales, aim, dh
             nc.scalar.copy(ta_sb[:, cols(c)], ta_ps[c][:])
 
         def dot(name, total, x, scalar, y):
-            terms = sb.tile([P, x.shape[1]], F32, name=name)
+            terms = sb.tile([P, x.shape[1]], F32, name=name, tag=name)
             nc.vector.scalar_tensor_tensor(terms[:], x, scalar, y, ALU.mult, ALU.mult, accum_out=total)
 
         z = sb.tile([P, 1], F32)
         rz = sb.tile([P, 1], F32)
         s1g = sb.tile([P, G], F32)
-        lin = sb.tile([P, 2], F32)
+        lin = sb.tile([P, 3], F32)
         sq = sb.tile([P, 2], F32)
-        crz, k, nk2, kc = col(lin, 0), col(lin, 1), col(sq, 0), col(sq, 1)
+        crz, k, nrz, nk2, kc = col(lin, 0), col(lin, 1), col(lin, 2), col(sq, 0), col(sq, 1)
         u = sb.tile([P, G], F32)
-        w_ext = sb.tile([P, G + 2], F32)
-        w = w_ext[:, 0:G]
-        dz = sb.tile([P, 1], F32)
-        mu = sb.tile([P, 1], F32)
+        w_ext = sb.tile([P, G + 1], F32)
+        w, us = w_ext[:, 0:G], col(w_ext, G)
+        y_ext = sb.tile([P, G + 1], F32)
+        y, neg_mu = y_ext[:, 0:G], col(y_ext, G)
         dz_fac = sb.tile([P, CHUNKS], F32)
-        wm = sb.tile([P, G], F32)
+        um = sb.tile([P, G], F32)
 
-        copy_ta(3)
-        copy_ta(2)
-        weigh(0)
-        copy_ta(0)
-        dot("z_terms", z[:], csum[:], 1.0, fac[:])
-        weigh(1)
-        copy_ta(1)
-        nc.vector.reciprocal(rz[:], z[:])
-        nc.vector.tensor_reduce(s1g[:], grouped(px[:]), AX.X, ALU.add)
-        nc.vector.tensor_scalar(lin[:], lin_consts[:], rz[:], None, ALU.mult)
-        nc.vector.tensor_scalar(sq[:], sq_consts[:], rz[:], rz[:], ALU.mult, ALU.mult)
-        weigh(2)
-        nc.vector.scalar_tensor_tensor(u[:], s1g[:], crz, aim_sb[:], ALU.mult, ALU.subtract)
-        nc.vector.scalar_tensor_tensor(w, s1g[:], k, aim_sb[:], ALU.mult, ALU.subtract)
-        weigh(3)
-        dot("dz_terms", dz[:], u[:], nk2, s1g[:])
-        dot("mu_terms", mu[:], xsum[:], rz[:], fac[:])
-        nc.vector.tensor_scalar(dz_fac[:], fac[:], dz[:], None, ALU.mult)
-        xpx = sb.tile([P, SLOTS], F32)
-        nc.vector.tensor_tensor(xpx[:], ta_sb[:].indirect(offsets[:]), px[:], ALU.mult)
-        dot("u_terms", col(w_ext, G), u[:], mu[:], s1g[:])
-        dot("w_terms", col(w_ext, G + 1), w, mu[:], s1g[:])
-        nc.vector.tensor_scalar(wm[:], w, mu[:], k, ALU.mult, ALU.mult)
+        def scaled_term(name, c, values, scale, last):
+            term = sb.tile([P, BANK], F32, name=f"{name}{c}", tag=f"{name}{c}")
+            nc.scalar.activation(term[:], values[:], ACT.Copy, scale=scale)
+            add_turned(c, term, last=last)
 
-        for c in range(CHUNKS):
-            term = sb.tile([P, BANK], F32, name=f"dz_term{c}")
-            nc.scalar.activation(term[:], xp[c][:], ACT.Copy, scale=col(dz_fac, c))
-            add_turned(c, term)
-
-        nc.vector.tensor_reduce(xs_ext[:, 0:G], grouped(xpx[:]), AX.X, ALU.add)
-        e2 = sb.tile([P, SLOTS], F32)
-        nc.vector.scalar_tensor_tensor(grouped(e2[:]), grouped(xpx[:]), k, spread(u[:]), ALU.mult, ALU.mult)
-        xdz = sb.tile([P, 1], F32)
-        dot("xdz_terms", xdz[:], xs_ext[:], nk2, w_ext[:])
-        xr = sb.tile([P, G], F32)
-        nc.vector.scalar_tensor_tensor(xr[:], xs_ext[:, 0:G], kc, wm[:], ALU.mult, ALU.subtract)
-        xdz_fac = sb.tile([P, CHUNKS], F32)
-        nc.vector.tensor_scalar(xdz_fac[:], fac[:], xdz[:], None, ALU.mult)
-        e1 = sb.tile([P, SLOTS], F32)
-        nc.vector.tensor_tensor(grouped(e1[:]), grouped(px[:]), spread(xr[:]), ALU.mult)
-        nc.vector.tensor_tensor(xs2[:].indirect(offsets[:]), e1[:], e2[:], ALU.add)
-
-        def last_term(c):
-            term = sb.tile([P, BANK], F32, name=f"xdz_term{c}")
-            nc.scalar.activation(term[:], p[c][:], ACT.Copy, scale=col(xdz_fac, c))
-            add_turned(c, term, last=True)
-
-        def finish(c):
-            held = sb.tile([P, BANK], F32, name=f"held{c}")
+        def leave_bank(c):
+            held = sb.tile([P, BANK], F32, name=f"held{c}", tag=f"held{c}")
             nc.scalar.copy(held[:], turned[c][:])
+            return held
+
+        def turn_back(c, held):
             dense = ps.tile([P, BANK], F32, name=f"dense{c}", tag=f"right{c}")
             for j in range(BLOCKS):
                 block = slice(j * P, (j + 1) * P)
                 nc.tensor.transpose(dense[:, block], held[:, block], ident[:])
-            result = sb.tile([P, BANK], F32, name=f"result{c}")
-            nc.vector.tensor_tensor(result[:], dense[:], xs2[:, cols(c)], ALU.add)
-            nc.sync.dma_start(out[:, cols(c)], result[:])
+            return dense
 
-        last_term(0)
-        for c in range(CHUNKS):
-            if c + 1 < CHUNKS:
-                last_term(c + 1)
-            finish(c)
+        def finish(c, dense, pieces):
+            for inside in pieces:
+                result = sb.tile([P, inside.stop - inside.start], F32, name=f"result{c}_{inside.start}")
+                nc.vector.tensor_tensor(result[:], dense[:, inside], xs2[:, cols(c)][:, inside], ALU.add)
+                nc.sync.dma_start(out[:, cols(c)][:, inside], result[:])
+
+        copy_ta(3)
+        copy_ta(2)
+        dot("z_terms", z[:], csum[:], 1.0, fac[:])
+        weigh(0)
+        copy_ta(0)
+        nc.vector.reciprocal(rz[:], z[:])
+        nc.vector.tensor_reduce(s1g[:], grouped(px[:]), AX.X, ALU.add)
+        nc.vector.tensor_scalar(lin[:], lin_consts[:], rz[:], None, ALU.mult)
+        nc.gpsimd.tensor_scalar(sq[:], sq_consts[:], rz[:], rz[:], ALU.mult, ALU.mult)
+        weigh(1)
+        copy_ta(1)
+        nc.vector.scalar_tensor_tensor(u[:], s1g[:], crz, aim_sb[:], ALU.mult, ALU.subtract)
+        nc.vector.scalar_tensor_tensor(w, s1g[:], k, aim_sb[:], ALU.mult, ALU.subtract)
+        dot("us_terms", us, u[:], 1.0, s1g[:])
+        nc.gpsimd.tensor_scalar(dz_fac[:], fac[:], nk2, us, ALU.mult, ALU.mult)
+        weigh(2)
+        weigh(3)
+        for c in range(direct):
+            scaled_term("dz_term", c, xp[c], col(dz_fac, c), last=False)
+
+        dot("mu_terms", neg_mu, xsum[:], nrz, fac[:])
+        xpx = sb.tile([P, SLOTS], F32)
+        nc.vector.tensor_tensor(xpx[:], ta_sb[:].indirect(offsets[:]), px[:], ALU.mult)
+
+        xs1g = sb.tile([P, G], F32, tag="xs1g")
+        nc.vector.tensor_reduce(xs1g[:], grouped(xpx[:]), AX.X, ALU.add)
+        nc.vector.tensor_scalar(um[:], u[:], neg_mu, k, ALU.mult, ALU.mult)
+        nc.vector.scalar_tensor_tensor(y, s1g[:], neg_mu, xs1g[:], ALU.mult, ALU.add)
+        yw = sb.tile([P, 1], F32)
+        dot("yw_terms", yw[:], y_ext[:], nk2, w_ext[:])
+        xdz_fac = sb.tile([P, CHUNKS], F32)
+        nc.scalar.activation(xdz_fac[:], fac[:], ACT.Copy, scale=yw[:])
+        xr = sb.tile([P, G], F32)
+        nc.vector.scalar_tensor_tensor(xr[:], y, kc, um[:], ALU.mult, ALU.add)
+        e2 = sb.tile([P, SLOTS], F32, tag="xs1g")
+        nc.vector.scalar_tensor_tensor(grouped(e2[:]), grouped(xpx[:]), k, spread(u[:]), ALU.mult, ALU.mult)
+        e1 = sb.tile([P, SLOTS], F32)
+        nc.vector.tensor_tensor(grouped(e1[:]), grouped(px[:]), spread(xr[:]), ALU.mult)
+        halves = (slice(0, BANK // 2), slice(BANK // 2, BANK))
+        early_direct = sb.tile([P, BANK], F32)
+        for inside in halves:
+            nc.vector.scalar_tensor_tensor(
+                early_direct[:, inside], xp[direct][:, inside], col(dz_fac, direct), base_sb[direct][:, inside],
+                ALU.mult, ALU.add,
+            )
+        nc.vector.tensor_tensor(xs2[:].indirect(offsets[:]), e1[:], e2[:], ALU.add)
+        def finish_direct():
+            rest = sb.tile([P, BANK], F32)
+            nc.gpsimd.tensor_tensor(rest[:], early_direct[:], xs2[:, cols(direct)], ALU.add)
+            result = sb.tile([P, BANK], F32, name="result_direct", tag=f"held{direct - 2}")
+            nc.vector.scalar_tensor_tensor(result[:], p[direct][:], col(xdz_fac, direct), rest[:], ALU.mult, ALU.add)
+            nc.sync.dma_start(out[:, cols(direct)], result[:])
+
+        scaled_term("xdz_term", 0, p[0], col(xdz_fac, 0), last=True)
+        for c in range(direct):
+            if c + 1 < direct:
+                scaled_term("xdz_term", c + 1, p[c + 1], col(xdz_fac, c + 1), last=True)
+                finish(c, turn_back(c, leave_bank(c)), [slice(0, BANK)])
+            else:
+                dense = turn_back(c, leave_bank(c))
+                finish_direct()
+                finish(c, dense, halves)

@@ -42,14 +42,17 @@ def tile_attend_hvgroupaims_heads_kernel(tc, hid, voc_words, voc_scales, aim, dh
             return ap.rearrange("p (g j) -> p g j", j=GROUP)
 
         def spread(ap):
-            return ap.unsqueeze(2).to_broadcast([P, G, GROUP])
+            return ap.unsqueeze(2).to_broadcast([P, ap.shape[1], GROUP])
 
         voc_plane = sb.tile([P, V], U8, align_bytes=64)
         nc.vector.memset(voc_plane[:].bitcast(I32), 0)
-        warm = sb.tile([P, 1], F32)
-        nc.gpsimd.memset(warm[:], 0.0)
-        warm_out = sb.tile([P, 1], F32)
-        nc.scalar.activation(warm_out[:], warm[:], ACT.Exp)
+
+        lin_consts = sb.tile([P, 3], F32)
+        nc.gpsimd.memset(lin_consts[:, 0:1], 256.0)
+        nc.gpsimd.memset(lin_consts[:, 1:2], 512.0)
+        nc.gpsimd.memset(lin_consts[:, 2:3], -1.0)
+        sq_consts = sb.tile([P, 3], F32)
+        nc.scalar.activation(sq_consts[:], lin_consts[:], ACT.Copy, scale=512.0)
 
         hid_raw = sb.tile([P, PACK, Q], F32)
         nc.sync.dma_start(hid_raw[:], hid.rearrange("(p t) q -> p t q", t=PACK))
@@ -58,11 +61,11 @@ def tile_attend_hvgroupaims_heads_kernel(tc, hid, voc_words, voc_scales, aim, dh
                 voc_plane[32 * quad : 32 * quad + 4, :].bitcast(I32),
                 voc_scales[0, 4 * quad : 4 * quad + 4, :].bitcast(I32),
             )
-        words = [sb.tile([P, 2 * BANK], U8, name=f"words{c}", align_bytes=64) for c in range(CHUNKS)]
-        for c in range(CHUNKS):
-            nc.sync.dma_start(words[c][:].bitcast(I32), voc_words[0, :, 2 * c * BANK : 2 * (c + 1) * BANK].bitcast(I32))
+        words = [sb.tile([P, V], U8, name=f"words{h}", align_bytes=64) for h in range(2)]
+        nc.sync.dma_start(words[0][:].bitcast(I32), voc_words[0, :, 0:V].bitcast(I32))
         dhid_raw = sb.tile([P, PACK, Q], F32)
         nc.sync.dma_start(dhid_raw[:], dhid.rearrange("(p t) q -> p t q", t=PACK))
+        nc.sync.dma_start(words[1][:].bitcast(I32), voc_words[0, :, V : 2 * V].bitcast(I32))
         offsets = sb.tile([P, SLOTS // 16], U16)
         nc.sync.dma_start(offsets[:], offs)
         aim_sb = sb.tile([P, G], F32, tag="aim")
@@ -75,14 +78,6 @@ def tile_attend_hvgroupaims_heads_kernel(tc, hid, voc_words, voc_scales, aim, dh
         make_identity(nc, ident[:])
         xs2 = sb.tile([P, V], F32)
         nc.vector.memset(xs2[:], 0.0)
-        lin_consts = sb.tile([P, 3], F32)
-        nc.gpsimd.memset(lin_consts[:, 0:1], 256.0)
-        nc.gpsimd.memset(lin_consts[:, 1:2], 512.0)
-        nc.gpsimd.memset(lin_consts[:, 2:3], -1.0)
-        sq_consts = sb.tile([P, 2], F32)
-        nc.gpsimd.memset(sq_consts[:, 0:1], -512.0)
-        nc.gpsimd.memset(sq_consts[:, 1:2], 131072.0)
-
         def interleaved(name):
             return sb.tile([P, Q * PACK], BF16, name=name, align_bytes=64)
 
@@ -112,7 +107,7 @@ def tile_attend_hvgroupaims_heads_kernel(tc, hid, voc_words, voc_scales, aim, dh
                 out=bank[:],
                 lhsT=codes[:].bitcast(FP8X4),
                 lhsT_scale=plane[:],
-                rhs=words[c][:].bitcast(FP4X4),
+                rhs=words[c // 2][:, 2 * BANK * (c % 2) : 2 * BANK * (c % 2 + 1)].bitcast(FP4X4),
                 rhs_scale=voc_plane[:, cols(c)],
                 start=True,
                 stop=True,
@@ -156,7 +151,7 @@ def tile_attend_hvgroupaims_heads_kernel(tc, hid, voc_words, voc_scales, aim, dh
         for c in range(direct):
             add_turned(c, base_sb[c], first=True)
 
-        xp_tags = ["xp0", "ax", "aim", "us_terms"]
+        xp_tags = ["xp0", "xp1", "ax", "aim"]
         xp = {}
         xsum = sb.tile([P, CHUNKS], F32)
         ta_sb = sb.tile([P, V], F32, tag="scores")
@@ -178,8 +173,8 @@ def tile_attend_hvgroupaims_heads_kernel(tc, hid, voc_words, voc_scales, aim, dh
         rz = sb.tile([P, 1], F32)
         s1g = sb.tile([P, G], F32)
         lin = sb.tile([P, 3], F32)
-        sq = sb.tile([P, 2], F32)
-        crz, k, nrz, nk2, kc = col(lin, 0), col(lin, 1), col(lin, 2), col(sq, 0), col(sq, 1)
+        sq = sb.tile([P, 3], F32)
+        crz, k, nrz, nk2, kc = col(lin, 0), col(lin, 1), col(lin, 2), col(sq, 2), col(sq, 0)
         u = sb.tile([P, G], F32)
         w_ext = sb.tile([P, G + 1], F32)
         w, us = w_ext[:, 0:G], col(w_ext, G)
@@ -211,33 +206,37 @@ def tile_attend_hvgroupaims_heads_kernel(tc, hid, voc_words, voc_scales, aim, dh
                 nc.vector.tensor_tensor(result[:], dense[:, inside], xs2[:, cols(c)][:, inside], ALU.add)
                 nc.sync.dma_start(out[:, cols(c)][:, inside], result[:])
 
-        copy_ta(3)
-        copy_ta(2)
-        dot("z_terms", z[:], csum[:], 1.0, fac[:])
         weigh(0)
         copy_ta(0)
+        dot("z_terms", z[:], csum[:], 1.0, fac[:])
+        weigh(1)
+        copy_ta(1)
+        copy_ta(3)
         nc.vector.reciprocal(rz[:], z[:])
         nc.vector.tensor_reduce(s1g[:], grouped(px[:]), AX.X, ALU.add)
         nc.vector.tensor_scalar(lin[:], lin_consts[:], rz[:], None, ALU.mult)
         nc.gpsimd.tensor_scalar(sq[:], sq_consts[:], rz[:], rz[:], ALU.mult, ALU.mult)
-        weigh(1)
-        copy_ta(1)
+        weigh(2)
+        copy_ta(2)
         nc.vector.scalar_tensor_tensor(u[:], s1g[:], crz, aim_sb[:], ALU.mult, ALU.subtract)
         nc.vector.scalar_tensor_tensor(w, s1g[:], k, aim_sb[:], ALU.mult, ALU.subtract)
         dot("us_terms", us, u[:], 1.0, s1g[:])
         nc.gpsimd.tensor_scalar(dz_fac[:], fac[:], nk2, us, ALU.mult, ALU.mult)
-        weigh(2)
+        r = sb.tile([P, G], F32, tag="us_terms")
+        nc.gpsimd.tensor_scalar(r[:], u[:], k, 0.0, ALU.mult, ALU.add)
         weigh(3)
         for c in range(direct):
             scaled_term("dz_term", c, xp[c], col(dz_fac, c), last=False)
+        dz_direct = sb.tile([P, BANK], F32)
+        nc.scalar.activation(dz_direct[:], xp[direct][:], ACT.Copy, scale=col(dz_fac, direct))
 
         dot("mu_terms", neg_mu, xsum[:], nrz, fac[:])
         xpx = sb.tile([P, SLOTS], F32)
         nc.vector.tensor_tensor(xpx[:], ta_sb[:].indirect(offsets[:]), px[:], ALU.mult)
 
-        xs1g = sb.tile([P, G], F32, tag="xs1g")
+        xs1g = sb.tile([P, G], F32)
         nc.vector.tensor_reduce(xs1g[:], grouped(xpx[:]), AX.X, ALU.add)
-        nc.vector.tensor_scalar(um[:], u[:], neg_mu, k, ALU.mult, ALU.mult)
+        nc.vector.tensor_scalar(um[:], r[:], neg_mu, None, ALU.mult)
         nc.vector.scalar_tensor_tensor(y, s1g[:], neg_mu, xs1g[:], ALU.mult, ALU.add)
         yw = sb.tile([P, 1], F32)
         dot("yw_terms", yw[:], y_ext[:], nk2, w_ext[:])
@@ -245,23 +244,24 @@ def tile_attend_hvgroupaims_heads_kernel(tc, hid, voc_words, voc_scales, aim, dh
         nc.scalar.activation(xdz_fac[:], fac[:], ACT.Copy, scale=yw[:])
         xr = sb.tile([P, G], F32)
         nc.vector.scalar_tensor_tensor(xr[:], y, kc, um[:], ALU.mult, ALU.add)
-        e2 = sb.tile([P, SLOTS], F32, tag="xs1g")
-        nc.vector.scalar_tensor_tensor(grouped(e2[:]), grouped(xpx[:]), k, spread(u[:]), ALU.mult, ALU.mult)
         e1 = sb.tile([P, SLOTS], F32)
         nc.vector.tensor_tensor(grouped(e1[:]), grouped(px[:]), spread(xr[:]), ALU.mult)
         halves = (slice(0, BANK // 2), slice(BANK // 2, BANK))
+        e2 = sb.tile([P, SLOTS], F32)
+        for inside in halves:
+            groups = slice(inside.start // GROUP, inside.stop // GROUP)
+            nc.vector.tensor_tensor(grouped(e2[:, inside]), grouped(xpx[:, inside]), spread(r[:, groups]), ALU.mult)
         early_direct = sb.tile([P, BANK], F32)
         for inside in halves:
-            nc.vector.scalar_tensor_tensor(
-                early_direct[:, inside], xp[direct][:, inside], col(dz_fac, direct), base_sb[direct][:, inside],
-                ALU.mult, ALU.add,
-            )
+            nc.vector.tensor_tensor(early_direct[:, inside], dz_direct[:, inside], base_sb[direct][:, inside], ALU.add)
         nc.vector.tensor_tensor(xs2[:].indirect(offsets[:]), e1[:], e2[:], ALU.add)
         def finish_direct():
             rest = sb.tile([P, BANK], F32)
             nc.gpsimd.tensor_tensor(rest[:], early_direct[:], xs2[:, cols(direct)], ALU.add)
+            term = sb.tile([P, BANK], F32, tag=f"xdz_term{direct - 1}")
+            nc.scalar.activation(term[:], p[direct][:], ACT.Copy, scale=col(xdz_fac, direct))
             result = sb.tile([P, BANK], F32, name="result_direct", tag=f"held{direct - 2}")
-            nc.vector.scalar_tensor_tensor(result[:], p[direct][:], col(xdz_fac, direct), rest[:], ALU.mult, ALU.add)
+            nc.vector.tensor_tensor(result[:], term[:], rest[:], ALU.add)
             nc.sync.dma_start(out[:, cols(direct)], result[:])
 
         scaled_term("xdz_term", 0, p[0], col(xdz_fac, 0), last=True)
@@ -272,4 +272,4 @@ def tile_attend_hvgroupaims_heads_kernel(tc, hid, voc_words, voc_scales, aim, dh
             else:
                 dense = turn_back(c, leave_bank(c))
                 finish_direct()
-                finish(c, dense, halves)
+                finish(c, dense, [slice(0, BANK - P), slice(BANK - P, BANK)])

from contextlib import ExitStack

import concourse.mybir as mybir
from concourse.masks import make_identity

D, V, Q, SLOTS, G = 512, 2048, 128, 512, 64
GROUP = SLOTS // G
FLOPS = 2 * 2 * D * Q * V

F32 = mybir.dt.float32
BF16 = mybir.dt.bfloat16
U32 = mybir.dt.uint32
I32 = mybir.dt.int32
U16 = mybir.dt.uint16
U8 = mybir.dt.uint8
FP8X4 = mybir.dt.float8_e4m3fn_x4
FP4X4 = mybir.dt.float4_e2m1fn_x4
ALU = mybir.AluOpType
ACT = mybir.ActivationFunctionType
AX = mybir.AxisListType

P = 128
PACK = 4
BANK = 512
CHUNKS = V // BANK
BLOCKS = BANK // P


def tile_attend_hvgroupaims_heads_kernel(tc, hid, voc_words, voc_scales, aim, dhid, base, offs, out):
    nc = tc.nc
    with ExitStack() as ctx:
        sb = ctx.enter_context(tc.tile_pool(name="sb", bufs=1))
        ps = ctx.enter_context(tc.psum_pool(name="ps", bufs=1))

        def cols(c):
            return slice(c * BANK, (c + 1) * BANK)

        def col(t, c):
            return t[:, c : c + 1]

        def grouped(ap):
            return ap.rearrange("p (g j) -> p g j", j=GROUP)

        def spread(ap):
            return ap.unsqueeze(2).to_broadcast([P, ap.shape[1], GROUP])

        voc_plane = sb.tile([P, V], U8, align_bytes=64)
        nc.vector.memset(voc_plane[:].bitcast(I32), 0)

        lin_consts = sb.tile([P, 3], F32)
        nc.gpsimd.memset(lin_consts[:, 0:1], 256.0)
        nc.gpsimd.memset(lin_consts[:, 1:2], 512.0)
        nc.gpsimd.memset(lin_consts[:, 2:3], -1.0)
        sq_consts = sb.tile([P, 3], F32)
        nc.scalar.activation(sq_consts[:], lin_consts[:], ACT.Copy, scale=512.0)

        hid_raw = sb.tile([P, PACK, Q], F32)
        nc.sync.dma_start(hid_raw[:], hid.rearrange("(p t) q -> p t q", t=PACK))
        for quad in range(4):
            nc.sync.dma_start(
                voc_plane[32 * quad : 32 * quad + 4, :].bitcast(I32),
                voc_scales[0, 4 * quad : 4 * quad + 4, :].bitcast(I32),
            )
        words = [sb.tile([P, V], U8, name=f"words{h}", align_bytes=64) for h in range(2)]
        nc.sync.dma_start(words[0][:].bitcast(I32), voc_words[0, :, 0:V].bitcast(I32))
        dhid_raw = sb.tile([P, PACK, Q], F32)
        nc.sync.dma_start(dhid_raw[:], dhid.rearrange("(p t) q -> p t q", t=PACK))
        nc.sync.dma_start(words[1][:].bitcast(I32), voc_words[0, :, V : 2 * V].bitcast(I32))
        offsets = sb.tile([P, SLOTS // 16], U16)
        nc.sync.dma_start(offsets[:], offs)
        aim_sb = sb.tile([P, G], F32, tag="aim")
        nc.sync.dma_start(aim_sb[:], aim)
        base_sb = [sb.tile([P, BANK], F32, name=f"base{c}") for c in range(CHUNKS)]
        for c in range(CHUNKS):
            nc.sync.dma_start(base_sb[c][:], base[:, cols(c)])

        ident = sb.tile([P, P], F32)
        make_identity(nc, ident[:])
        xs2 = sb.tile([P, V], F32)
        nc.vector.memset(xs2[:], 0.0)
        def interleaved(name):
            return sb.tile([P, Q * PACK], BF16, name=name, align_bytes=64)

        def as_written(t):
            return t[:].rearrange("p (c i t) -> p c t i", i=4, t=PACK)

        def as_read(raw):
            return raw[:].rearrange("p t (c i) -> p c t i", i=4)

        def quantise(name, bf):
            codes = sb.tile([P, Q], U32, name=name + "_codes", align_bytes=64)
            plane = sb.tile([P, Q], U8, name=name + "_plane", align_bytes=64)
            nc.vector.quantize_mx(out=codes[:].bitcast(FP8X4), scales=plane[:], in_=bf[:])
            return codes, plane

        hid_bf = interleaved("hid_bf")
        nc.vector.tensor_copy(as_written(hid_bf), as_read(hid_raw))
        dhid_bf = interleaved("dhid_bf")
        nc.scalar.copy(as_written(dhid_bf), as_read(dhid_raw))
        hid_q = quantise("hid", hid_bf)
        dhid_q = quantise("dhid", dhid_bf)

        def scores(name, operand, c):
            bank = ps.tile([P, BANK], F32, name=f"{name}{c}", tag=f"{name}{c}")
            codes, plane = operand
            nc.tensor.matmul_mx(
                out=bank[:],
                lhsT=codes[:].bitcast(FP8X4),
                lhsT_scale=plane[:],
                rhs=words[c // 2][:, 2 * BANK * (c % 2) : 2 * BANK * (c % 2 + 1)].bitcast(FP4X4),
                rhs_scale=voc_plane[:, cols(c)],
                start=True,
                stop=True,
            )
            return bank

        a_ps = [scores("left", hid_q, c) for c in range(CHUNKS)]
        ta_ps = [scores("right", dhid_q, c) for c in range(CHUNKS)]

        a_sb = sb.tile([P, V], F32, tag="scores")
        cmax = sb.tile([P, CHUNKS], F32)
        neg_run = sb.tile([P, CHUNKS], F32)
        csum = sb.tile([P, CHUNKS], F32)
        p = [sb.tile([P, BANK], F32, name=f"p{c}") for c in range(CHUNKS)]
        for c in range(CHUNKS):
            nc.vector.tensor_scalar(a_sb[:, cols(c)], a_ps[c][:], 1.0, None, ALU.mult, ALU.max, accum_out=col(cmax, c))
            if c == 0:
                nc.gpsimd.tensor_scalar(col(neg_run, c), col(cmax, c), -1.0, 0.0, ALU.mult, ALU.add)
            else:
                nc.gpsimd.tensor_scalar(col(neg_run, c), col(cmax, c), -1.0, col(neg_run, c - 1), ALU.mult, ALU.min)
            nc.scalar.activation(p[c][:], a_sb[:, cols(c)], ACT.Exp, bias=col(neg_run, c), accum_out=col(csum, c))
        neg_max = col(neg_run, CHUNKS - 1)
        ax = sb.tile([P, SLOTS], F32, tag="ax")
        nc.vector.tensor_copy(ax[:], a_sb[:].indirect(offsets[:]))
        fac = sb.tile([P, CHUNKS], F32)
        nc.scalar.activation(fac[:], neg_run[:], ACT.Exp, bias=neg_max, scale=-1.0)
        px = sb.tile([P, SLOTS], F32)
        nc.scalar.activation(px[:], ax[:], ACT.Exp, bias=neg_max)

        direct = CHUNKS - 1
        turned = [ps.tile([P, BANK], F32, name=f"turned{c}", tag=f"left{c}") for c in range(direct)]

        def add_turned(c, term, first=False, last=False):
            for j in range(BLOCKS):
                block = slice(j * P, (j + 1) * P)
                nc.tensor.matmul(
                    turned[c][:, block], lhsT=term[:, block], rhs=ident[:], is_transpose=True,
                    start=(first and j == 0), stop=(last and j == BLOCKS - 1),
                )

        for c in range(direct):
            add_turned(c, base_sb[c], first=True)

        xp_tags = ["xp0", "xp1", "ax", "aim"]
        xp = {}
        xsum = sb.tile([P, CHUNKS], F32)
        ta_sb = sb.tile([P, V], F32, tag="scores")

        def weigh(c):
            xp[c] = sb.tile([P, BANK], F32, name=f"xp{c}", tag=xp_tags[c])
            nc.vector.scalar_tensor_tensor(
                xp[c][:], ta_ps[c][:], 1.0, p[c][:], ALU.mult, ALU.mult, accum_out=col(xsum, c)
            )

        def copy_ta(c):
            nc.scalar.copy(ta_sb[:, cols(c)], ta_ps[c][:])

        def dot(name, total, x, scalar, y):
            terms = sb.tile([P, x.shape[1]], F32, name=name, tag=name)
            nc.vector.scalar_tensor_tensor(terms[:], x, scalar, y, ALU.mult, ALU.mult, accum_out=total)

        z = sb.tile([P, 1], F32)
        rz = sb.tile([P, 1], F32)
        s1g = sb.tile([P, G], F32)
        lin = sb.tile([P, 3], F32)
        sq = sb.tile([P, 3], F32)
        crz, k, nrz, nk2, kc = col(lin, 0), col(lin, 1), col(lin, 2), col(sq, 2), col(sq, 0)
        u = sb.tile([P, G], F32)
        w_ext = sb.tile([P, G + 1], F32)
        w, us = w_ext[:, 0:G], col(w_ext, G)
        y_ext = sb.tile([P, G + 1], F32)
        y, neg_mu = y_ext[:, 0:G], col(y_ext, G)
        dz_fac = sb.tile([P, CHUNKS], F32)
        um = sb.tile([P, G], F32)

        def scaled_term(name, c, values, scale, last):
            term = sb.tile([P, BANK], F32, name=f"{name}{c}", tag=f"{name}{c}")
            nc.scalar.activation(term[:], values[:], ACT.Copy, scale=scale)
            add_turned(c, term, last=last)

        def leave_bank(c):
            held = sb.tile([P, BANK], F32, name=f"held{c}", tag=f"held{c}")
            nc.scalar.copy(held[:], turned[c][:])
            return held

        def turn_back(c, held):
            dense = ps.tile([P, BANK], F32, name=f"dense{c}", tag=f"right{c}")
            for j in range(BLOCKS):
                block = slice(j * P, (j + 1) * P)
                nc.tensor.transpose(dense[:, block], held[:, block], ident[:])
            return dense

        def finish(c, dense, pieces):
            for inside in pieces:
                result = sb.tile([P, inside.stop - inside.start], F32, name=f"result{c}_{inside.start}")
                nc.vector.tensor_tensor(result[:], dense[:, inside], xs2[:, cols(c)][:, inside], ALU.add)
                nc.sync.dma_start(out[:, cols(c)][:, inside], result[:])

        weigh(0)
        copy_ta(0)
        dot("z_terms", z[:], csum[:], 1.0, fac[:])
        weigh(1)
        copy_ta(1)
        copy_ta(3)
        nc.vector.reciprocal(rz[:], z[:])
        nc.vector.tensor_reduce(s1g[:], grouped(px[:]), AX.X, ALU.add)
        nc.vector.tensor_scalar(lin[:], lin_consts[:], rz[:], None, ALU.mult)
        nc.gpsimd.tensor_scalar(sq[:], sq_consts[:], rz[:], rz[:], ALU.mult, ALU.mult)
        weigh(2)
        copy_ta(2)
        nc.vector.scalar_tensor_tensor(u[:], s1g[:], crz, aim_sb[:], ALU.mult, ALU.subtract)
        nc.vector.scalar_tensor_tensor(w, s1g[:], k, aim_sb[:], ALU.mult, ALU.subtract)
        dot("us_terms", us, u[:], 1.0, s1g[:])
        nc.gpsimd.tensor_scalar(dz_fac[:], fac[:], nk2, us, ALU.mult, ALU.mult)
        r = sb.tile([P, G], F32, tag="us_terms")
        nc.gpsimd.tensor_scalar(r[:], u[:], k, 0.0, ALU.mult, ALU.add)
        weigh(3)
        for c in range(direct):
            scaled_term("dz_term", c, xp[c], col(dz_fac, c), last=False)
        dz_direct = sb.tile([P, BANK], F32)
        nc.scalar.activation(dz_direct[:], xp[direct][:], ACT.Copy, scale=col(dz_fac, direct))

        dot("mu_terms", neg_mu, xsum[:], nrz, fac[:])
        xpx = sb.tile([P, SLOTS], F32)
        nc.vector.tensor_tensor(xpx[:], ta_sb[:].indirect(offsets[:]), px[:], ALU.mult)

        xs1g = sb.tile([P, G], F32)
        nc.vector.tensor_reduce(xs1g[:], grouped(xpx[:]), AX.X, ALU.add)
        nc.vector.tensor_scalar(um[:], r[:], neg_mu, None, ALU.mult)
        nc.vector.scalar_tensor_tensor(y, s1g[:], neg_mu, xs1g[:], ALU.mult, ALU.add)
        yw = sb.tile([P, 1], F32)
        dot("yw_terms", yw[:], y_ext[:], nk2, w_ext[:])
        xdz_fac = sb.tile([P, CHUNKS], F32)
        nc.scalar.activation(xdz_fac[:], fac[:], ACT.Copy, scale=yw[:])
        xr = sb.tile([P, G], F32)
        nc.vector.scalar_tensor_tensor(xr[:], y, kc, um[:], ALU.mult, ALU.add)
        e1 = sb.tile([P, SLOTS], F32)
        nc.vector.tensor_tensor(grouped(e1[:]), grouped(px[:]), spread(xr[:]), ALU.mult)
        halves = (slice(0, BANK // 2), slice(BANK // 2, BANK))
        e2 = sb.tile([P, SLOTS], F32)
        for inside in halves:
            groups = slice(inside.start // GROUP, inside.stop // GROUP)
            nc.vector.tensor_tensor(grouped(e2[:, inside]), grouped(xpx[:, inside]), spread(r[:, groups]), ALU.mult)
        early_direct = sb.tile([P, BANK], F32)
        for inside in halves:
            nc.vector.tensor_tensor(early_direct[:, inside], dz_direct[:, inside], base_sb[direct][:, inside], ALU.add)
        nc.vector.tensor_tensor(xs2[:].indirect(offsets[:]), e1[:], e2[:], ALU.add)
        def finish_direct():
            rest = sb.tile([P, BANK], F32)
            nc.gpsimd.tensor_tensor(rest[:], early_direct[:], xs2[:, cols(direct)], ALU.add)
            term = sb.tile([P, BANK], F32, tag=f"xdz_term{direct - 1}")
            nc.scalar.activation(term[:], p[direct][:], ACT.Copy, scale=col(xdz_fac, direct))
            result = sb.tile([P, BANK], F32, name="result_direct", tag=f"held{direct - 2}")
            nc.vector.tensor_tensor(result[:], term[:], rest[:], ALU.add)
            nc.sync.dma_start(out[:, cols(direct)], result[:])

        scaled_term("xdz_term", 0, p[0], col(xdz_fac, 0), last=True)
        for c in range(direct):
            if c + 1 < direct:
                scaled_term("xdz_term", c + 1, p[c + 1], col(xdz_fac, c + 1), last=True)
                finish(c, turn_back(c, leave_bank(c)), [slice(0, BANK)])
            else:
                dense = turn_back(c, leave_bank(c))
                finish_direct()
                finish(c, dense, [slice(0, BANK - P), slice(BANK - P, BANK)])
